import numpy as np, ml_dtypes
CORES = [24,26,29,31,48,50,53,55]
N = 8
import mx_ref
NC, NZ = 256, 128
BF = ml_dtypes.bfloat16
def setup_inputs(rng):
    def f(*shape):
        return mx_ref.flush((rng.standard_normal(shape, dtype=np.float32) * np.exp2(rng.integers(-2, 3, shape[:-1] + (1,)))).astype(BF))
    return {"w": f(N, 128, 512), "x": f(N, 128, 4 * NC), "d": f(N, 128, N * 512), "z": f(N, 128, 4 * NZ)}
def setup_inputs_blocks(rng):
    d = setup_inputs(rng)
    for k in ("w", "x", "d", "z"): d[k] = mx_ref.spread(d[k], rng, 2)
    return d
def setup_inputs_wide(rng):
    d = setup_inputs(rng)
    for k in ("w", "x", "d", "z"): d[k] = mx_ref.flush((d[k].astype(np.float32) * np.exp2(rng.integers(-8, 9, (N, 1, 1))).astype(np.float32)).astype(BF))
    return d
def setup_inputs_zeros(rng):
    d = setup_inputs(rng); v = d["x"].reshape(N, 128, -1, 4).copy()
    v[np.broadcast_to((rng.random((N, 1, v.shape[2], 1)) < 0.33), v.shape)] = 0
    d["x"] = v.reshape(d["x"].shape)
    return d
def reference(w, x, d, z):
    QX = [mx_ref.quantize(x[j]) for j in range(N)]; QZ = [mx_ref.quantize(z[j]) for j in range(N)]
    y = np.zeros((N, 128, N * NC), np.float32); h = np.zeros((N, 128, NZ), np.float32)
    for r in range(N):
        qw = mx_ref.quantize(w[r])
        for j in range(N):
            y[r][:, NC * j:NC * j + NC] = mx_ref.matmul(qw, QX[j])
            p = mx_ref.matmul(mx_ref.quantize(d[r][:, 512 * j:512 * j + 512]), QZ[j])
            h[r] = p if j == 0 else h[r] + p
    return {"y": y, "h": h}

@@ -1,0 +1,166 @@
+from concourse.bass import DstId, RemoteDMATransfer
+from concourse.mybir import dt, ActivationFunctionType
+
+N = 8
+XW, ZW, TW = 256, 128, 128
+SL = XW + ZW
+BANK = 512
+YB = 7
+
+SCRATCH = {
+    "xb": ("sbuf", [128, 4 * XW], "bfloat16"),
+    "zb": ("sbuf", [128, 4 * ZW], "bfloat16"),
+    "wb": ("sbuf", [128, 4 * TW], "bfloat16"),
+    "db": ("sbuf", [128, 4 * TW * N], "bfloat16"),
+    "qc": ("sbuf", [128, SL * N], "float8_e4m3fn_x4"),
+    "qs": ("sbuf", [128, SL * N], "uint8"),
+    "wc": ("sbuf", [128, TW], "float8_e4m3fn_x4"),
+    "ws": ("sbuf", [128, TW], "uint8"),
+    "dc": ("sbuf", [128, TW * N], "float8_e4m3fn_x4"),
+    "ds": ("sbuf", [128, TW * N], "uint8"),
+    "ysb": ("sbuf", [128, XW * N], "float32"),
+    "hsb": ("sbuf", [128, ZW], "float32"),
+    "ps": ("psum", [128, BANK * (YB + 1)], "float32"),
+}
+SEMAPHORES = (["ldx", "ldz", "ldw", "ldd0", "ldd1", "q", "qw", "qd", "sent", "sta", "stb", "mh", "ch"]
+              + ["ac%d" % j for j in range(N)] + ["as%d" % j for j in range(N)]
+              + ["my%d" % i for i in range(N)] + ["cy%d" % i for i in range(N)])
+
+
+def _bits(m):
+    return bin(m).count("1")
+
+
+def _plan(cores, topo):
+    sends = {c: [] for c in cores}
+    count, when = {}, {}
+
+    def add(c, prio, j, wait, groups, keys):
+        sends[c].append((prio, j, wait, groups))
+        for (dests, mask), key in zip(groups, keys):
+            for t in dests:
+                count[(t, j)] = _bits(mask)
+                when[(t, j)] = key
+
+    for j, s in enumerate(cores):
+        near = [c for c in cores if c != s and topo.chip(c) == topo.chip(s)]
+        far = [c for c in cores if topo.chip(c) != topo.chip(s)]
+        if topo.may_write(s, far[0]):
+            gate = s
+        else:
+            gate = [c for c in near if topo.die(c) == topo.die(s) and topo.may_write(c, far[0])][0]
+        side = [c for c in far if topo.die(c) == topo.die(gate)]
+        land = [c for c in side if topo.may_write(c, s) == (gate != s)][0]
+        out = topo.mask(gate, land)
+        if gate == s:
+            add(s, 0, j, False, [([land], out), (near, topo.mask(s, near[0]) & ~out)], [2, 5])
+        else:
+            add(s, 0, j, False, [([gate], topo.mask(s, gate))], [0])
+            rest = [c for c in near if c != gate]
+            add(s, 1, j, False, [(rest, topo.mask(s, rest[0]))], [1])
+            add(gate, 2, j, True, [([land], out)], [4])
+        rest = [c for c in far if c != land]
+        add(land, 3, j, True, [(rest, topo.mask(land, rest[0]))], [6 if gate == s else 7])
+    for c in cores:
+        sends[c].sort(key=lambda e: e[0])
+    return sends, count, when
+
+
+def rank_program(g, core, T, topo):
+    rank = T.rank_of(core)
+    if rank is None:
+        return
+    cores = list(T.cores)
+    sem = T.sem
+    sends, count, when = _plan(cores, topo)
+    own = SL * rank
+
+    half = 2 * TW * N
+    g.sync.dma_start(T.xb[:], T.x[:]).then_inc(sem.ldx, 16)
+    g.scalar.dma_start(T.zb[:], T.z[:]).then_inc(sem.ldz, 16)
+    g.scalar.dma_start(T.wb[:], T.w[:]).then_inc(sem.ldw, 16)
+    g.sync.dma_start(T.db[:, 0:half], T.d[:, 0:half]).then_inc(sem.ldd0, 16)
+    g.scalar.dma_start(T.db[:, half:2 * half], T.d[:, half:2 * half]).then_inc(sem.ldd1, 16)
+
+    v = g.vector
+    v.wait_ge(sem.ldz, 16)
+    v.quantize_mx(T.qc[:, own + XW:own + SL], T.qs[:, own + XW:own + SL], T.zb[:]).then_inc(sem.q, 1)
+    v.wait_ge(sem.ldx, 16)
+    v.quantize_mx(T.qc[:, own:own + XW], T.qs[:, own:own + XW], T.xb[:]).then_inc(sem.q, 1)
+    v.wait_ge(sem.ldw, 16)
+    v.quantize_mx(T.wc[:], T.ws[:], T.wb[:]).then_inc(sem.qw, 1)
+    hw = TW * N // 2
+    v.wait_ge(sem.ldd0, 16)
+    v.quantize_mx(T.dc[:, 0:hw], T.ds[:, 0:hw], T.db[:, 0:half]).then_inc(sem.qd, 1)
+    v.wait_ge(sem.ldd1, 16)
+    v.quantize_mx(T.dc[:, hw:2 * hw], T.ds[:, hw:2 * hw], T.db[:, half:2 * half]).then_inc(sem.qd, 1)
+
+    sent = 0
+    g.wait_ge(sem.q, 2)
+    for _, j, wait, groups in sends[core]:
+        a, b = SL * j, SL * (j + 1)
+        for kind in ("ac", "as"):
+            arrived = sem["%s%d" % (kind, j)]
+            if wait:
+                g.wait_ge(arrived, count[(core, j)])
+            trs = []
+            for dests, mask in groups:
+                if kind == "ac":
+                    src = T.qc[:, a:b].bitcast(dt.uint8)
+                    dsts = [T.qc[:, a:b].bitcast(dt.uint8) for _ in dests]
+                else:
+                    src = T.qs[:, a:b]
+                    dsts = [T.qs[:, a:b] for _ in dests]
+                ids = [DstId(rid=topo.addr(t)[0], pnc=topo.addr(t)[1]) for t in dests]
+                trs.append(RemoteDMATransfer(dst_ids=ids, dma_engine_mask=mask, remote_sem=arrived,
+                                             srcs=[src], dsts=dsts))
+                sent += _bits(mask)
+            g.remote_dma_fused(trs, local_sem=sem.sent)
+    g.wait_ge(sem.sent, sent)
+
+    order = [rank] + sorted((j for j in range(N) if j != rank), key=lambda j: (when[(core, j)], j))
+    te = g.tensor
+    hb = BANK * YB
+    te.wait_ge(sem.qw, 1)
+    for i, j in enumerate(order):
+        if j == rank:
+            te.wait_ge(sem.q, 2)
+        else:
+            te.wait_ge(sem["ac%d" % j], count[(core, j)])
+            te.wait_ge(sem["as%d" % j], count[(core, j)])
+        if i >= YB:
+            te.wait_ge(sem["cy%d" % (i - YB)], 1)
+        p = BANK * (i % YB)
+        a = SL * j
+        te.matmul_mx(T.ps[:, p:p + XW], T.wc[:], T.ws[:], T.qc[:, a:a + XW], T.qs[:, a:a + XW],
+                     True, True).then_inc(sem["my%d" % i], 1)
+        if i == 0:
+            te.wait_ge(sem.qd, 2)
+        mm = te.matmul_mx(T.ps[:, hb:hb + ZW], T.dc[:, TW * j:TW * (j + 1)], T.ds[:, TW * j:TW * (j + 1)],
+                          T.qc[:, a + XW:a + SL], T.qs[:, a + XW:a + SL], i == 0, i == N - 1)
+        if i == N - 1:
+            mm.then_inc(sem.mh, 1)
+
+    stored = {"sta": 0, "stb": 0}
+    for i, j in enumerate(order):
+        p = BANK * (i % YB)
+        c0 = XW * j
+        if i % 2 == 0:
+            v.wait_ge(sem["my%d" % i], 1)
+            v.tensor_copy(T.ysb[:, c0:c0 + XW], T.ps[:, p:p + XW]).then_inc(sem["cy%d" % i], 1)
+            q, st = g.sync, "sta"
+        else:
+            g.scalar.wait_ge(sem["my%d" % i], 1)
+            g.scalar.activation(T.ysb[:, c0:c0 + XW], T.ps[:, p:p + XW],
+                                ActivationFunctionType.Copy).then_inc(sem["cy%d" % i], 1)
+            q, st = g.scalar, "stb"
+        q.wait_ge(sem["cy%d" % i], 1)
+        q.dma_start(T.y[:, c0:c0 + XW], T.ysb[:, c0:c0 + XW]).then_inc(sem[st], 16)
+        stored[st] += 16
+    v.wait_ge(sem.mh, 1)
+    v.tensor_copy(T.hsb[:], T.ps[:, hb:hb + ZW]).then_inc(sem.ch, 1)
+    g.sync.wait_ge(sem.ch, 1)
+    g.sync.dma_start(T.h[:], T.hsb[:]).then_inc(sem.sta, 16)
+    stored["sta"] += 16
+    g.sync.wait_ge(sem.sta, stored["sta"])
+    g.scalar.wait_ge(sem.stb, stored["stb"])

@@ -2,10 +2,12 @@ from concourse.bass import DstId, RemoteDMATransfer
 from concourse.mybir import dt, ActivationFunctionType
 
 N = 8
+NCORES = 64
 XW, ZW, TW = 256, 128, 128
 SL = XW + ZW
 BANK = 512
 YB = 7
+ZC, XC, PL = 0, 1, 2
 
 SCRATCH = {
     "xb": ("sbuf", [128, 4 * XW], "bfloat16"),
@@ -22,8 +24,8 @@ SCRATCH = {
     "hsb": ("sbuf", [128, ZW], "float32"),
     "ps": ("psum", [128, BANK * (YB + 1)], "float32"),
 }
-SEMAPHORES = (["ldx", "ldz", "ldw", "ldd0", "ldd1", "q", "qw", "qd", "sent", "sta", "stb", "mh", "ch"]
-              + ["ac%d" % j for j in range(N)] + ["as%d" % j for j in range(N)]
+SEMAPHORES = (["ldx", "ldz", "ldw", "ldd0", "ldd1", "qz", "qx", "qw", "qd0", "qd1", "sent", "sta", "stb", "mh", "ch"]
+              + ["a%dp%d" % (j, p) for j in range(N) for p in (ZC, XC, PL)]
               + ["my%d" % i for i in range(N)] + ["cy%d" % i for i in range(N)])
 
 
@@ -32,15 +34,18 @@ def _bits(m):
 
 
 def _plan(cores, topo):
-    sends = {c: [] for c in cores}
-    count, when = {}, {}
+    sends, count, when = {}, {}, {}
 
-    def add(c, prio, j, wait, groups, keys):
-        sends[c].append((prio, j, wait, groups))
+    def add(c, prio, j, p, wait, groups, keys):
+        sends.setdefault(c, []).append((prio, p, j, wait, groups))
         for (dests, mask), key in zip(groups, keys):
             for t in dests:
-                count[(t, j)] = _bits(mask)
-                when[(t, j)] = key
+                count[(t, j, p)] = _bits(mask)
+                when[(t, j)] = max(key, when.get((t, j), 0))
+
+    def spread(c, prio, j, p, far, key):
+        rest = [t for t in far if t != c]
+        add(c, prio, j, p, True, [(rest, topo.mask(c, rest[0]))], [key])
 
     for j, s in enumerate(cores):
         near = [c for c in cores if c != s and topo.chip(c) == topo.chip(s)]
@@ -50,92 +55,120 @@ def _plan(cores, topo):
         else:
             gate = [c for c in near if topo.die(c) == topo.die(s) and topo.may_write(c, far[0])][0]
         side = [c for c in far if topo.die(c) == topo.die(gate)]
-        land = [c for c in side if topo.may_write(c, s) == (gate != s)][0]
-        out = topo.mask(gate, land)
+        lg = [c for c in side if topo.may_write(c, s)][0]
+        ln = [c for c in side if not topo.may_write(c, s)][0]
         if gate == s:
-            add(s, 0, j, False, [([land], out), (near, topo.mask(s, near[0]) & ~out)], [2, 5])
+            out = topo.mask(s, ln)
+            for p in (ZC, XC, PL):
+                add(s, 0, j, p, False, [([ln], out), (near, topo.mask(s, near[0]) & ~out)], [5, 2])
+                spread(ln, 3, j, p, far, 6)
         else:
-            add(s, 0, j, False, [([gate], topo.mask(s, gate))], [0])
+            aide = [c for c in range(NCORES) if c not in cores and topo.chip(c) == topo.chip(s)
+                    and topo.die(c) == topo.die(gate) and topo.may_write(c, far[0])][0]
             rest = [c for c in near if c != gate]
-            add(s, 1, j, False, [(rest, topo.mask(s, rest[0]))], [1])
-            add(gate, 2, j, True, [([land], out)], [4])
-        rest = [c for c in far if c != land]
-        add(land, 3, j, True, [(rest, topo.mask(land, rest[0]))], [6 if gate == s else 7])
-    for c in cores:
-        sends[c].sort(key=lambda e: e[0])
+            for p in (ZC, XC, PL):
+                first = [gate] if p == XC else [gate, aide]
+                add(s, 0, j, p, False, [(first, topo.mask(s, gate))], [0])
+                add(s, 1, j, p, False, [(rest, topo.mask(s, rest[0]))], [1])
+                carrier, land = (gate, lg) if p == XC else (aide, ln)
+                add(carrier, 2, j, p, True, [([land], topo.mask(carrier, land))], [7])
+                spread(land, 4, j, p, far, 7)
+    for c in sends:
+        sends[c].sort(key=lambda e: e[:3])
     return sends, count, when
 
 
+def _piece(T, j, p):
+    a = SL * j
+    if p == XC:
+        return T.qc[:, a:a + XW].bitcast(dt.uint8)
+    if p == ZC:
+        return T.qc[:, a + XW:a + SL].bitcast(dt.uint8)
+    return T.qs[:, a:a + SL]
+
+
+def _send_all(g, core, T, topo, sends, count):
+    sem = T.sem
+    sent = 0
+    have = set()
+    for _, p, j, wait, groups in sends.get(core, []):
+        arrived = sem["a%dp%d" % (j, p)]
+        if wait:
+            g.wait_ge(arrived, count[(core, j, p)])
+        else:
+            for need in (("qz",) if p == ZC else ("qx",) if p == XC else ("qz", "qx")):
+                if need not in have:
+                    g.wait_ge(sem[need], 1)
+                    have.add(need)
+        trs = []
+        for dests, mask in groups:
+            ids = [DstId(rid=topo.addr(t)[0], pnc=topo.addr(t)[1]) for t in dests]
+            trs.append(RemoteDMATransfer(dst_ids=ids, dma_engine_mask=mask, remote_sem=arrived,
+                                         srcs=[_piece(T, j, p)], dsts=[_piece(T, j, p) for _ in dests]))
+            sent += _bits(mask)
+        g.remote_dma_fused(trs, local_sem=sem.sent)
+    if sent:
+        g.wait_ge(sem.sent, sent)
+
+
 def rank_program(g, core, T, topo):
+    cores = list(T.cores)
+    sends, count, when = _plan(cores, topo)
     rank = T.rank_of(core)
     if rank is None:
+        _send_all(g, core, T, topo, sends, count)
         return
-    cores = list(T.cores)
     sem = T.sem
-    sends, count, when = _plan(cores, topo)
     own = SL * rank
 
     half = 2 * TW * N
-    g.sync.dma_start(T.xb[:], T.x[:]).then_inc(sem.ldx, 16)
-    g.scalar.dma_start(T.zb[:], T.z[:]).then_inc(sem.ldz, 16)
-    g.scalar.dma_start(T.wb[:], T.w[:]).then_inc(sem.ldw, 16)
-    g.sync.dma_start(T.db[:, 0:half], T.d[:, 0:half]).then_inc(sem.ldd0, 16)
-    g.scalar.dma_start(T.db[:, half:2 * half], T.d[:, half:2 * half]).then_inc(sem.ldd1, 16)
+    hw = TW * N // 2
+    ha = 2 * rank // N
+    hz = 1 - ha
+    g.sync.dma_start(T.zb[:], T.z[:]).then_inc(sem.ldz, 16)
+    g.scalar.dma_start(T.xb[:], T.x[:]).then_inc(sem.ldx, 16)
+    g.sync.dma_start(T.wb[:], T.w[:]).then_inc(sem.ldw, 16)
+    g.scalar.dma_start(T.db[:, half * ha:half * (ha + 1)], T.d[:, half * ha:half * (ha + 1)]).then_inc(
+        sem["ldd%d" % ha], 16)
+    g.sync.dma_start(T.db[:, half * hz:half * (hz + 1)], T.d[:, half * hz:half * (hz + 1)]).then_inc(
+        sem["ldd%d" % hz], 16)
 
     v = g.vector
     v.wait_ge(sem.ldz, 16)
-    v.quantize_mx(T.qc[:, own + XW:own + SL], T.qs[:, own + XW:own + SL], T.zb[:]).then_inc(sem.q, 1)
+    v.quantize_mx(T.qc[:, own + XW:own + SL], T.qs[:, own + XW:own + SL], T.zb[:]).then_inc(sem.qz, 1)
     v.wait_ge(sem.ldx, 16)
-    v.quantize_mx(T.qc[:, own:own + XW], T.qs[:, own:own + XW], T.xb[:]).then_inc(sem.q, 1)
+    v.quantize_mx(T.qc[:, own:own + XW], T.qs[:, own:own + XW], T.xb[:]).then_inc(sem.qx, 1)
     v.wait_ge(sem.ldw, 16)
     v.quantize_mx(T.wc[:], T.ws[:], T.wb[:]).then_inc(sem.qw, 1)
-    hw = TW * N // 2
-    v.wait_ge(sem.ldd0, 16)
-    v.quantize_mx(T.dc[:, 0:hw], T.ds[:, 0:hw], T.db[:, 0:half]).then_inc(sem.qd, 1)
-    v.wait_ge(sem.ldd1, 16)
-    v.quantize_mx(T.dc[:, hw:2 * hw], T.ds[:, hw:2 * hw], T.db[:, half:2 * half]).then_inc(sem.qd, 1)
+    for k in (ha, hz):
+        v.wait_ge(sem["ldd%d" % k], 16)
+        v.quantize_mx(T.dc[:, hw * k:hw * (k + 1)], T.ds[:, hw * k:hw * (k + 1)],
+                      T.db[:, half * k:half * (k + 1)]).then_inc(sem["qd%d" % k], 1)
 
-    sent = 0
-    g.wait_ge(sem.q, 2)
-    for _, j, wait, groups in sends[core]:
-        a, b = SL * j, SL * (j + 1)
-        for kind in ("ac", "as"):
-            arrived = sem["%s%d" % (kind, j)]
-            if wait:
-                g.wait_ge(arrived, count[(core, j)])
-            trs = []
-            for dests, mask in groups:
-                if kind == "ac":
-                    src = T.qc[:, a:b].bitcast(dt.uint8)
-                    dsts = [T.qc[:, a:b].bitcast(dt.uint8) for _ in dests]
-                else:
-                    src = T.qs[:, a:b]
-                    dsts = [T.qs[:, a:b] for _ in dests]
-                ids = [DstId(rid=topo.addr(t)[0], pnc=topo.addr(t)[1]) for t in dests]
-                trs.append(RemoteDMATransfer(dst_ids=ids, dma_engine_mask=mask, remote_sem=arrived,
-                                             srcs=[src], dsts=dsts))
-                sent += _bits(mask)
-            g.remote_dma_fused(trs, local_sem=sem.sent)
-    g.wait_ge(sem.sent, sent)
+    _send_all(g, core, T, topo, sends, count)
 
     order = [rank] + sorted((j for j in range(N) if j != rank), key=lambda j: (when[(core, j)], j))
     te = g.tensor
     hb = BANK * YB
+    dready = set()
     te.wait_ge(sem.qw, 1)
     for i, j in enumerate(order):
         if j == rank:
-            te.wait_ge(sem.q, 2)
+            te.wait_ge(sem.qz, 1)
+            te.wait_ge(sem.qx, 1)
         else:
-            te.wait_ge(sem["ac%d" % j], count[(core, j)])
-            te.wait_ge(sem["as%d" % j], count[(core, j)])
+            for p in (ZC, XC, PL):
+                te.wait_ge(sem["a%dp%d" % (j, p)], count[(core, j, p)])
         if i >= YB:
             te.wait_ge(sem["cy%d" % (i - YB)], 1)
         p = BANK * (i % YB)
         a = SL * j
         te.matmul_mx(T.ps[:, p:p + XW], T.wc[:], T.ws[:], T.qc[:, a:a + XW], T.qs[:, a:a + XW],
                      True, True).then_inc(sem["my%d" % i], 1)
-        if i == 0:
-            te.wait_ge(sem.qd, 2)
+        k = 2 * j // N
+        if k not in dready:
+            te.wait_ge(sem["qd%d" % k], 1)
+            dready.add(k)
         mm = te.matmul_mx(T.ps[:, hb:hb + ZW], T.dc[:, TW * j:TW * (j + 1)], T.ds[:, TW * j:TW * (j + 1)],
                           T.qc[:, a + XW:a + SL], T.qs[:, a + XW:a + SL], i == 0, i == N - 1)
         if i == N - 1:

from concourse.bass import DstId, RemoteDMATransfer
from concourse.mybir import dt, ActivationFunctionType

N = 8
NCORES = 64
XW, ZW, TW = 256, 128, 128
SL = XW + ZW
BANK = 512
YB = 7
ZC, XC, PL = 0, 1, 2

SCRATCH = {
    "xb": ("sbuf", [128, 4 * XW], "bfloat16"),
    "zb": ("sbuf", [128, 4 * ZW], "bfloat16"),
    "wb": ("sbuf", [128, 4 * TW], "bfloat16"),
    "db": ("sbuf", [128, 4 * TW * N], "bfloat16"),
    "qc": ("sbuf", [128, SL * N], "float8_e4m3fn_x4"),
    "qs": ("sbuf", [128, SL * N], "uint8"),
    "wc": ("sbuf", [128, TW], "float8_e4m3fn_x4"),
    "ws": ("sbuf", [128, TW], "uint8"),
    "dc": ("sbuf", [128, TW * N], "float8_e4m3fn_x4"),
    "ds": ("sbuf", [128, TW * N], "uint8"),
    "ysb": ("sbuf", [128, XW * N], "float32"),
    "hsb": ("sbuf", [128, ZW], "float32"),
    "ps": ("psum", [128, BANK * (YB + 1)], "float32"),
}
SEMAPHORES = (["ldx", "ldz", "ldw", "ldd0", "ldd1", "qz", "qx", "qw", "qd0", "qd1", "sent", "sta", "stb", "mh", "ch"]
              + ["a%dp%d" % (j, p) for j in range(N) for p in (ZC, XC, PL)]
              + ["my%d" % i for i in range(N)] + ["cy%d" % i for i in range(N)])


def _bits(m):
    return bin(m).count("1")


def _plan(cores, topo):
    sends, count, when = {}, {}, {}

    def add(c, prio, j, p, wait, groups, keys):
        sends.setdefault(c, []).append((prio, p, j, wait, groups))
        for (dests, mask), key in zip(groups, keys):
            for t in dests:
                count[(t, j, p)] = _bits(mask)
                when[(t, j)] = max(key, when.get((t, j), 0))

    def spread(c, prio, j, p, far, key):
        rest = [t for t in far if t != c]
        add(c, prio, j, p, True, [(rest, topo.mask(c, rest[0]))], [key])

    for j, s in enumerate(cores):
        near = [c for c in cores if c != s and topo.chip(c) == topo.chip(s)]
        far = [c for c in cores if topo.chip(c) != topo.chip(s)]
        if topo.may_write(s, far[0]):
            gate = s
        else:
            gate = [c for c in near if topo.die(c) == topo.die(s) and topo.may_write(c, far[0])][0]
        side = [c for c in far if topo.die(c) == topo.die(gate)]
        lg = [c for c in side if topo.may_write(c, s)][0]
        ln = [c for c in side if not topo.may_write(c, s)][0]
        if gate == s:
            out = topo.mask(s, ln)
            for p in (ZC, XC, PL):
                add(s, 0, j, p, False, [([ln], out), (near, topo.mask(s, near[0]) & ~out)], [5, 2])
                spread(ln, 3, j, p, far, 6)
        else:
            aide = [c for c in range(NCORES) if c not in cores and topo.chip(c) == topo.chip(s)
                    and topo.die(c) == topo.die(gate) and topo.may_write(c, far[0])][0]
            rest = [c for c in near if c != gate]
            for p in (ZC, XC, PL):
                first = [gate] if p == XC else [gate, aide]
                add(s, 0, j, p, False, [(first, topo.mask(s, gate))], [0])
                add(s, 1, j, p, False, [(rest, topo.mask(s, rest[0]))], [1])
                carrier, land = (gate, lg) if p == XC else (aide, ln)
                add(carrier, 2, j, p, True, [([land], topo.mask(carrier, land))], [7])
                spread(land, 4, j, p, far, 7)
    for c in sends:
        sends[c].sort(key=lambda e: e[:3])
    return sends, count, when


def _piece(T, j, p):
    a = SL * j
    if p == XC:
        return T.qc[:, a:a + XW].bitcast(dt.uint8)
    if p == ZC:
        return T.qc[:, a + XW:a + SL].bitcast(dt.uint8)
    return T.qs[:, a:a + SL]


def _send_all(g, core, T, topo, sends, count):
    sem = T.sem
    sent = 0
    have = set()
    for _, p, j, wait, groups in sends.get(core, []):
        arrived = sem["a%dp%d" % (j, p)]
        if wait:
            g.wait_ge(arrived, count[(core, j, p)])
        else:
            for need in (("qz",) if p == ZC else ("qx",) if p == XC else ("qz", "qx")):
                if need not in have:
                    g.wait_ge(sem[need], 1)
                    have.add(need)
        trs = []
        for dests, mask in groups:
            ids = [DstId(rid=topo.addr(t)[0], pnc=topo.addr(t)[1]) for t in dests]
            trs.append(RemoteDMATransfer(dst_ids=ids, dma_engine_mask=mask, remote_sem=arrived,
                                         srcs=[_piece(T, j, p)], dsts=[_piece(T, j, p) for _ in dests]))
            sent += _bits(mask)
        g.remote_dma_fused(trs, local_sem=sem.sent)
    if sent:
        g.wait_ge(sem.sent, sent)


def rank_program(g, core, T, topo):
    cores = list(T.cores)
    sends, count, when = _plan(cores, topo)
    rank = T.rank_of(core)
    if rank is None:
        _send_all(g, core, T, topo, sends, count)
        return
    sem = T.sem
    own = SL * rank

    half = 2 * TW * N
    hw = TW * N // 2
    ha = 2 * rank // N
    hz = 1 - ha
    g.sync.dma_start(T.zb[:], T.z[:]).then_inc(sem.ldz, 16)
    g.scalar.dma_start(T.xb[:], T.x[:]).then_inc(sem.ldx, 16)
    g.sync.dma_start(T.wb[:], T.w[:]).then_inc(sem.ldw, 16)
    g.scalar.dma_start(T.db[:, half * ha:half * (ha + 1)], T.d[:, half * ha:half * (ha + 1)]).then_inc(
        sem["ldd%d" % ha], 16)
    g.sync.dma_start(T.db[:, half * hz:half * (hz + 1)], T.d[:, half * hz:half * (hz + 1)]).then_inc(
        sem["ldd%d" % hz], 16)

    v = g.vector
    v.wait_ge(sem.ldz, 16)
    v.quantize_mx(T.qc[:, own + XW:own + SL], T.qs[:, own + XW:own + SL], T.zb[:]).then_inc(sem.qz, 1)
    v.wait_ge(sem.ldx, 16)
    v.quantize_mx(T.qc[:, own:own + XW], T.qs[:, own:own + XW], T.xb[:]).then_inc(sem.qx, 1)
    v.wait_ge(sem.ldw, 16)
    v.quantize_mx(T.wc[:], T.ws[:], T.wb[:]).then_inc(sem.qw, 1)
    for k in (ha, hz):
        v.wait_ge(sem["ldd%d" % k], 16)
        v.quantize_mx(T.dc[:, hw * k:hw * (k + 1)], T.ds[:, hw * k:hw * (k + 1)],
                      T.db[:, half * k:half * (k + 1)]).then_inc(sem["qd%d" % k], 1)

    _send_all(g, core, T, topo, sends, count)

    order = [rank] + sorted((j for j in range(N) if j != rank), key=lambda j: (when[(core, j)], j))
    te = g.tensor
    hb = BANK * YB
    dready = set()
    te.wait_ge(sem.qw, 1)
    for i, j in enumerate(order):
        if j == rank:
            te.wait_ge(sem.qz, 1)
            te.wait_ge(sem.qx, 1)
        else:
            for p in (ZC, XC, PL):
                te.wait_ge(sem["a%dp%d" % (j, p)], count[(core, j, p)])
        if i >= YB:
            te.wait_ge(sem["cy%d" % (i - YB)], 1)
        p = BANK * (i % YB)
        a = SL * j
        te.matmul_mx(T.ps[:, p:p + XW], T.wc[:], T.ws[:], T.qc[:, a:a + XW], T.qs[:, a:a + XW],
                     True, True).then_inc(sem["my%d" % i], 1)
        k = 2 * j // N
        if k not in dready:
            te.wait_ge(sem["qd%d" % k], 1)
            dready.add(k)
        mm = te.matmul_mx(T.ps[:, hb:hb + ZW], T.dc[:, TW * j:TW * (j + 1)], T.ds[:, TW * j:TW * (j + 1)],
                          T.qc[:, a + XW:a + SL], T.qs[:, a + XW:a + SL], i == 0, i == N - 1)
        if i == N - 1:
            mm.then_inc(sem.mh, 1)

    stored = {"sta": 0, "stb": 0}
    for i, j in enumerate(order):
        p = BANK * (i % YB)
        c0 = XW * j
        if i % 2 == 0:
            v.wait_ge(sem["my%d" % i], 1)
            v.tensor_copy(T.ysb[:, c0:c0 + XW], T.ps[:, p:p + XW]).then_inc(sem["cy%d" % i], 1)
            q, st = g.sync, "sta"
        else:
            g.scalar.wait_ge(sem["my%d" % i], 1)
            g.scalar.activation(T.ysb[:, c0:c0 + XW], T.ps[:, p:p + XW],
                                ActivationFunctionType.Copy).then_inc(sem["cy%d" % i], 1)
            q, st = g.scalar, "stb"
        q.wait_ge(sem["cy%d" % i], 1)
        q.dma_start(T.y[:, c0:c0 + XW], T.ysb[:, c0:c0 + XW]).then_inc(sem[st], 16)
        stored[st] += 16
    v.wait_ge(sem.mh, 1)
    v.tensor_copy(T.hsb[:], T.ps[:, hb:hb + ZW]).then_inc(sem.ch, 1)
    g.sync.wait_ge(sem.ch, 1)
    g.sync.dma_start(T.h[:], T.hsb[:]).then_inc(sem.sta, 16)
    stored["sta"] += 16
    g.sync.wait_ge(sem.sta, stored["sta"])
    g.scalar.wait_ge(sem.stb, stored["stb"])
